import numpy as np
import ml_dtypes


def mxq(x, axis, fmt="e4m3"):
    dtype, down = {"e4m3": (ml_dtypes.float8_e4m3fn, 7), "e5m2": (ml_dtypes.float8_e5m2, 14)}[fmt]
    v = np.moveaxis(np.asarray(x, np.float32).astype(ml_dtypes.bfloat16).astype(np.float64), axis, -1)
    blocks = v.reshape(v.shape[:-1] + (-1, 32))
    amax = np.abs(blocks).max(-1, keepdims=True)
    byte = np.maximum(np.where(amax > 0, np.frexp(amax)[1] - 1 + 127, 0) - down, 1)
    scale = np.exp2(byte - 127.0)
    codes = (blocks / scale).astype(np.float32).astype(dtype).astype(np.float64)
    return np.moveaxis((codes * scale).reshape(v.shape), -1, axis)


WIDE = False


def mx_kscale(k):
    if not WIDE:
        return np.ones(k)
    levels = np.array([10, -10, 5, -5, 0])
    if k % 512:
        return np.exp2(np.random.permutation(np.resize(levels, k // 32))).repeat(32)
    a = np.empty((k // 512, 16))
    for p in range(k // 512):
        a[p, :8] = np.random.permutation(np.resize(levels, 8))
        for g in range(8):
            far = levels[np.abs(levels - a[p, g]) >= 10]
            a[p, g + 8] = far[np.random.randint(len(far))]
    return np.exp2(a.ravel()).repeat(32)


def f64(x):
    return np.asarray(x).astype(np.float64)


def striped(idx):
    return np.tile(np.asarray(idx).reshape(-1, 16).T, (8, 1)).astype(np.uint16)


def unstriped(offs):
    return offs[:16].T.reshape(-1).astype(np.int64)


E2M1 = np.array([0.0, 0.5, 1.0, 1.5, 2.0, 3.0, 4.0, 6.0, -0.0, -0.5, -1.0, -1.5, -2.0, -3.0, -4.0, -6.0])


def pack_weight(w, fmt):
    k, n = w.shape
    w = f64(np.asarray(w, np.float32).astype(ml_dtypes.bfloat16)).reshape(k // 32, 32, n)
    amax = np.abs(w).max(1)
    if fmt == "e4m3":
        byte = np.frexp(amax)[1] - 1 + 127 - 7
    else:
        mant, ex = np.frexp(amax / 6.0)
        byte = np.where(mant > 0.5, ex, ex - 1) + 127
    byte = np.clip(np.where(amax > 0, byte, 1), 1, 254)
    scaled = (w * np.exp2(127.0 - byte)[:, None, :]).reshape(k, n).astype(np.float32)
    by_word = np.ascontiguousarray(scaled.reshape(k // 512, 128, 4, n).transpose(0, 1, 3, 2))
    if fmt == "e4m3":
        words = by_word.astype(ml_dtypes.float8_e4m3fn).view(np.uint8)
    else:
        c = by_word.astype(ml_dtypes.float4_e2m1fn).view(np.uint8) & 0xF
        words = (c[..., 0::2] | (c[..., 1::2] << 4)).reshape(k // 512, 128, 2 * n)
    return np.ascontiguousarray(words), np.ascontiguousarray(byte.astype(np.uint8).reshape(k // 512, 16, n))


def unpack_weight(words, scales, fmt):
    g, _, n = scales.shape
    words = np.ascontiguousarray(words).reshape(g, 128, n, -1)
    if fmt == "e4m3":
        vals = words.view(ml_dtypes.float8_e4m3fn).astype(np.float64)
    else:
        nib = np.empty((g, 128, n, 4), np.uint8)
        nib[..., 0::2] = words & 0xF
        nib[..., 1::2] = words >> 4
        vals = E2M1[nib]
    vals = vals * np.repeat(np.exp2(scales.astype(np.float64) - 127.0), 8, axis=1)[..., None]
    return vals.transpose(0, 1, 3, 2).reshape(g * 512, n)


D, E, T, I, Q = 512, 512, 2048, 512, 128


def setup_inputs():
    n = np.random.standard_normal
    idx = np.random.permutation(T)[:I]
    fd = mx_kscale(D)
    fi = mx_kscale(I)
    ti = np.ones(T)
    ti[idx] = fi
    keysp = pack_weight(n((D, T)) / fd[:, None], "e2m1")
    return {
        "query": (n((D, Q)) * 0.7 / np.sqrt(D) * fd[:, None]).astype(np.float32),
        "keys_words": keysp[0],
        "keys_scales": keysp[1],
        "dquery": (n((D, Q)) * 0.6 / np.sqrt(D) * fd[:, None]).astype(np.float32),
        "os": (np.random.uniform(0.2, 0.8, (1, I)) * fi).astype(np.float32),
        "vals": (n((E, T)) / ti).astype(np.float32),
        "offs": striped(idx),
    }


def reference(query, keys_words, keys_scales, dquery, os, vals, offs):
    idx = unstriped(offs)
    keysu = unpack_weight(keys_words, keys_scales, "e2m1")
    queryq = mxq(f64(query), 0, "e4m3")
    keysidxg = keysu[:, idx]
    a = queryq.T @ keysidxg
    dqueryq = mxq(f64(dquery), 0, "e4m3")
    ta = dqueryq.T @ keysidxg
    p = np.exp(a - np.max(a, axis=1, keepdims=True))
    n2 = np.sqrt(np.sum(np.square(p), axis=1, keepdims=True))
    tp = ta * p
    tn2 = np.sum(tp * p * 2.0, axis=1, keepdims=True) * 0.5 / n2
    tw = (tp - tn2 * p / n2) / n2
    wo1 = tw * f64(os)
    wt1 = wo1.T
    vt1 = f64(vals)[:, idx].T
    wt1q = mxq(wt1, 0, "e4m3")
    vt1q = mxq(vt1, 0, "e4m3")
    o = wt1q.T @ vt1q
    return o

@@ -1,0 +1,200 @@
+from contextlib import ExitStack
+
+import concourse.mybir as mybir
+from concourse.masks import make_identity
+
+D, E, T, I, Q = 512, 512, 2048, 512, 128
+FLOPS = 2 * Q * I * D * 2 + 2 * Q * I * E
+
+F32 = mybir.dt.float32
+BF16 = mybir.dt.bfloat16
+I32 = mybir.dt.int32
+U32 = mybir.dt.uint32
+U16 = mybir.dt.uint16
+U8 = mybir.dt.uint8
+FP8X4 = mybir.dt.float8_e4m3fn_x4
+FP4X4 = mybir.dt.float4_e2m1fn_x4
+ALU = mybir.AluOpType
+ACT = mybir.ActivationFunctionType
+
+P = 128
+PACK = 4
+LIST_ROWS = 16
+E_TILES = E // P
+VECTOR_SLOTS = (0, 0, 256, 256)
+
+
+def tile_attend_ttunitweights_kernel(tc, query, keys_words, keys_scales, dquery, slot_factor, vals, offs, out):
+    nc = tc.nc
+    with ExitStack() as ctx:
+        keep = ctx.enter_context(tc.tile_pool(name="keep", bufs=1))
+        psum = ctx.enter_context(tc.psum_pool(name="psum", bufs=1))
+
+        def sbuf(shape, dtype, name, tag=None):
+            return keep.tile(shape, dtype, name=name, tag=tag or name, align_bytes=64)
+
+        def quantize(grouped, columns, name, tag=None):
+            codes = sbuf([P, columns], U32, name + "_codes", tag)
+            scales = sbuf([P, columns], U8, name + "_scales")
+            nc.vector.quantize_mx(out=codes[:].bitcast(FP8X4), scales=scales[:], in_=grouped)
+            return codes, scales
+
+        def turn(rows, name, tag):
+            bank = psum.tile([P, 2, P], F32, name=name, tag=tag)
+            pairs = rows[:].bitcast(F32)
+            for u in range(2):
+                nc.tensor.transpose(bank[:, u, :], pairs[:, u : I // 2 : 2], ident[:])
+            return bank[:].rearrange("s u c -> s c u")
+
+        offsets = keep.tile([P, I // LIST_ROWS], U16, name="offsets")
+        nc.sync.dma_start(offsets[:], offs)
+        key_pool = sbuf([P, T], U16, "key_pool")
+        nc.sync.dma_start(key_pool[:].bitcast(I32), keys_words[0].bitcast(I32))
+        key_scale_pool = sbuf([P, T], U8, "key_scale_pool")
+        nc.vector.memset(key_scale_pool[:].bitcast(I32), 0)
+        for quad in range(4):
+            nc.sync.dma_start(
+                key_scale_pool[32 * quad : 32 * quad + 4, :].bitcast(I32),
+                keys_scales[0, 4 * quad : 4 * quad + 4, :].bitcast(I32),
+            )
+        q_raw = []
+        for n, src in enumerate((query, dquery)):
+            raw = sbuf([P, PACK, Q], F32, f"q_raw{n}")
+            nc.sync.dma_start(raw[:], src.rearrange("(p t) q -> p t q", t=PACK))
+            q_raw.append(raw)
+        val_pool = []
+        for j in range(E_TILES):
+            pool_j = sbuf([P, T], F32, f"val_pool{j}")
+            nc.sync.dma_start(pool_j[:], vals[j * P : (j + 1) * P, :])
+            val_pool.append(pool_j)
+        factor = sbuf([P, PACK], F32, "factor")
+        nc.gpsimd.dma_start(factor[:], slot_factor[0].rearrange("(s t) -> s t", t=PACK))
+
+        ident = sbuf([P, P], F32, "ident")
+        make_identity(nc, ident[:])
+        minus_half = sbuf([P, 1], F32, "minus_half")
+        nc.gpsimd.memset(minus_half[:], -0.5)
+
+        factor_bank = psum.tile([Q, PACK, P], F32, name="factor_bank", tag="bank_f")
+        for t in range(PACK):
+            nc.tensor.transpose(factor_bank[:, t, :], factor[:, t : t + 1].to_broadcast([P, Q]), ident[:])
+
+        key_words = sbuf([P, I], U16, "key_words")
+        nc.vector.tensor_copy(key_words[:], key_pool[:].indirect(offsets[:]))
+        key_scales = sbuf([P, I], U8, "key_scales")
+        nc.vector.tensor_copy(key_scales[:], key_scale_pool[:].indirect(offsets[:]))
+
+        q_grouped = sbuf([P, 2, Q, PACK], BF16, "q_grouped")
+        for n in range(2):
+            nc.scalar.copy(q_grouped[:, n, :, :], q_raw[n][:].rearrange("p t q -> p q t"))
+        q_codes, q_scales = quantize(q_grouped[:].rearrange("p n q t -> p (n q t)"), 2 * Q, "q")
+        banks = []
+        for n in range(2):
+            bank = psum.tile([Q, I], F32, name=f"score{n}", tag=f"bank_s{n}")
+            nc.tensor.matmul_mx(
+                out=bank[:],
+                lhsT=q_codes[:, n * Q : (n + 1) * Q].bitcast(FP8X4),
+                lhsT_scale=q_scales[:, n * Q : (n + 1) * Q],
+                rhs=key_words[:].bitcast(FP4X4),
+                rhs_scale=key_scales[:],
+                start=True,
+                stop=True,
+            )
+            banks.append(bank)
+        a_bank, ta_bank = banks
+
+        def gather_values(j, tag):
+            picked = sbuf([P, I], BF16, f"picked{j}", tag)
+            share = VECTOR_SLOTS[j]
+            cut = share // LIST_ROWS
+            if share > 0:
+                nc.vector.tensor_copy(picked[:, :share], val_pool[j][:].indirect(offsets[:, :cut]))
+            nc.scalar.activation(picked[:, share:], val_pool[j][:].indirect(offsets[:, cut:]), ACT.Copy)
+            return picked
+
+        picked0 = gather_values(0, None)
+
+        a_m2 = sbuf([Q, I], F32, "a_m2")
+        top_m2 = sbuf([Q, 1], F32, "top_m2")
+        nc.vector.tensor_scalar(a_m2[:], a_bank[:], -2.0, None, ALU.mult, ALU.min, accum_out=top_m2[:])
+        p_sq = sbuf([Q, I], F32, "p_sq", "val_pool0")
+        sum_sq = sbuf([Q, 1], F32, "sum_sq")
+        nc.scalar.activation(p_sq[:], a_m2[:], ACT.Exp, bias=top_m2[:], scale=-1.0, accum_out=sum_sq[:])
+        top_m1 = sbuf([Q, 1], F32, "top_m1")
+        nc.vector.tensor_scalar(top_m1[:], top_m2[:], 0.5, None, ALU.mult)
+        p = sbuf([Q, I], F32, "p")
+        nc.scalar.activation(p[:], a_m2[:], ACT.Exp, bias=top_m1[:], scale=-0.5)
+
+        turned0 = turn(picked0, "turned0", "bank_s0")
+        picked1 = gather_values(1, "a_m2")
+        turned1 = turn(picked1, "turned1", "bank_t1")
+
+        inv_n2 = sbuf([Q, 1], F32, "inv_n2")
+        nc.gpsimd.tensor_tensor(inv_n2[:], sum_sq[:], minus_half[:], ALU.pow)
+        ta_p_sq = sbuf([Q, I], F32, "ta_p_sq")
+        sum_ta = sbuf([Q, 1], F32, "sum_ta")
+        nc.vector.scalar_tensor_tensor(ta_p_sq[:], ta_bank[:], 1.0, p_sq[:], ALU.mult, ALU.mult, accum_out=sum_ta[:])
+        p_unit = sbuf([Q, P, PACK], F32, "p_unit")
+        nc.vector.scalar_tensor_tensor(
+            p_unit[:],
+            p[:].rearrange("q (s t) -> q s t", t=PACK),
+            inv_n2[:],
+            factor_bank[:].rearrange("q t s -> q s t"),
+            ALU.mult,
+            ALU.mult,
+        )
+        mean_ta = sbuf([Q, 1], F32, "mean_ta")
+        nc.vector.tensor_scalar(mean_ta[:], sum_ta[:], inv_n2[:], inv_n2[:], ALU.mult, ALU.mult)
+        wo = sbuf([Q, I], BF16, "wo", "val_pool1")
+        nc.vector.scalar_tensor_tensor(
+            wo[:], ta_bank[:], mean_ta[:], p_unit[:].rearrange("q s t -> q (s t)"), ALU.subtract, ALU.mult
+        )
+        turned_w = turn(wo, "turned_w", "bank_w")
+
+        picked2 = gather_values(2, "p_unit")
+        turned2 = turn(picked2, "turned2", "bank_t2")
+        early = sbuf([P, 3, P, 2], F32, "early_grouped", "val_pool2")
+        nc.scalar.copy(early[:, 0, :, :], turned0)
+        nc.scalar.copy(early[:, 1, :, :], turned1)
+        nc.vector.tensor_copy(early[:, 2, :, :], turned_w)
+        early_codes, early_scales = quantize(
+            early[:].rearrange("s n c u -> s (n c u)").bitcast(BF16), 3 * P, "early"
+        )
+        grouped2 = sbuf([P, P, 2], F32, "grouped2")
+        nc.scalar.copy(grouped2[:], turned2)
+
+        def product(bank, codes, scales):
+            nc.tensor.matmul_mx(
+                out=bank,
+                lhsT=early_codes[:, 2 * P :].bitcast(FP8X4),
+                lhsT_scale=early_scales[:, 2 * P :],
+                rhs=codes.bitcast(FP8X4),
+                rhs_scale=scales,
+                start=True,
+                stop=True,
+            )
+
+        bank01 = psum.tile([Q, 2 * P], F32, name="bank01", tag="bank_f")
+        product(bank01[:], early_codes[:, : 2 * P], early_scales[:, : 2 * P])
+
+        picked3 = gather_values(3, "val_pool2")
+        turned3 = turn(picked3, "turned3", "bank_t3")
+        grouped3 = sbuf([P, P, 2], F32, "grouped3")
+        nc.scalar.copy(grouped3[:], turned3)
+
+        codes2, scales2 = quantize(grouped2[:].rearrange("s c u -> s (c u)").bitcast(BF16), P, "v2", "val_pool3")
+        bank2 = psum.tile([Q, P], F32, name="bank2", tag="bank_s1")
+        product(bank2[:], codes2[:], scales2[:])
+        out01 = sbuf([Q, 2 * P], F32, "out01", "grouped2")
+        nc.vector.tensor_copy(out01[:], bank01[:])
+        nc.sync.dma_start(out[:, : 2 * P], out01[:])
+
+        codes3, scales3 = quantize(grouped3[:].rearrange("s c u -> s (c u)").bitcast(BF16), P, "v3")
+        bank3 = psum.tile([Q, P], F32, name="bank3")
+        product(bank3[:], codes3[:], scales3[:])
+        out2 = sbuf([Q, P], F32, "out2")
+        nc.scalar.copy(out2[:], bank2[:])
+        nc.sync.dma_start(out[:, 2 * P : 3 * P], out2[:])
+        out3 = sbuf([Q, P], F32, "out3")
+        nc.scalar.copy(out3[:], bank3[:])
+        nc.sync.dma_start(out[:, 3 * P :], out3[:])

@@ -21,7 +21,7 @@ P = 128
 PACK = 4
 LIST_ROWS = 16
 E_TILES = E // P
-VECTOR_SLOTS = (0, 0, 256, 256)
+VECTOR_SLOTS = (512, 0, 256, 256)
 
 
 def tile_attend_ttunitweights_kernel(tc, query, keys_words, keys_scales, dquery, slot_factor, vals, offs, out):
@@ -84,17 +84,16 @@ def tile_attend_ttunitweights_kernel(tc, query, keys_words, keys_scales, dquery,
         key_scales = sbuf([P, I], U8, "key_scales")
         nc.vector.tensor_copy(key_scales[:], key_scale_pool[:].indirect(offsets[:]))
 
-        q_grouped = sbuf([P, 2, Q, PACK], BF16, "q_grouped")
-        for n in range(2):
-            nc.scalar.copy(q_grouped[:, n, :, :], q_raw[n][:].rearrange("p t q -> p q t"))
-        q_codes, q_scales = quantize(q_grouped[:].rearrange("p n q t -> p (n q t)"), 2 * Q, "q")
         banks = []
         for n in range(2):
+            q_grouped = sbuf([P, Q, PACK], BF16, f"q_grouped{n}")
+            nc.scalar.copy(q_grouped[:], q_raw[n][:].rearrange("p t q -> p q t"))
+            q_codes, q_scales = quantize(q_grouped[:].rearrange("p q t -> p (q t)"), Q, f"q{n}")
             bank = psum.tile([Q, I], F32, name=f"score{n}", tag=f"bank_s{n}")
             nc.tensor.matmul_mx(
                 out=bank[:],
-                lhsT=q_codes[:, n * Q : (n + 1) * Q].bitcast(FP8X4),
-                lhsT_scale=q_scales[:, n * Q : (n + 1) * Q],
+                lhsT=q_codes[:].bitcast(FP8X4),
+                lhsT_scale=q_scales[:],
                 rhs=key_words[:].bitcast(FP4X4),
                 rhs_scale=key_scales[:],
                 start=True,
@@ -109,15 +108,14 @@ def tile_attend_ttunitweights_kernel(tc, query, keys_words, keys_scales, dquery,
             cut = share // LIST_ROWS
             if share > 0:
                 nc.vector.tensor_copy(picked[:, :share], val_pool[j][:].indirect(offsets[:, :cut]))
-            nc.scalar.activation(picked[:, share:], val_pool[j][:].indirect(offsets[:, cut:]), ACT.Copy)
+            if share < I:
+                nc.scalar.activation(picked[:, share:], val_pool[j][:].indirect(offsets[:, cut:]), ACT.Copy)
             return picked
-
-        picked0 = gather_values(0, None)
 
         a_m2 = sbuf([Q, I], F32, "a_m2")
         top_m2 = sbuf([Q, 1], F32, "top_m2")
         nc.vector.tensor_scalar(a_m2[:], a_bank[:], -2.0, None, ALU.mult, ALU.min, accum_out=top_m2[:])
-        p_sq = sbuf([Q, I], F32, "p_sq", "val_pool0")
+        p_sq = sbuf([Q, I], F32, "p_sq")
         sum_sq = sbuf([Q, 1], F32, "sum_sq")
         nc.scalar.activation(p_sq[:], a_m2[:], ACT.Exp, bias=top_m2[:], scale=-1.0, accum_out=sum_sq[:])
         top_m1 = sbuf([Q, 1], F32, "top_m1")
@@ -125,13 +123,17 @@ def tile_attend_ttunitweights_kernel(tc, query, keys_words, keys_scales, dquery,
         p = sbuf([Q, I], F32, "p")
         nc.scalar.activation(p[:], a_m2[:], ACT.Exp, bias=top_m1[:], scale=-0.5)
 
+        picked0 = gather_values(0, "key_words")
         turned0 = turn(picked0, "turned0", "bank_s0")
         picked1 = gather_values(1, "a_m2")
         turned1 = turn(picked1, "turned1", "bank_t1")
+        grouped01 = sbuf([P, 2, P, 2], F32, "grouped01", "val_pool1")
+        nc.scalar.copy(grouped01[:, 0, :, :], turned0)
+        nc.scalar.copy(grouped01[:, 1, :, :], turned1)
 
         inv_n2 = sbuf([Q, 1], F32, "inv_n2")
         nc.gpsimd.tensor_tensor(inv_n2[:], sum_sq[:], minus_half[:], ALU.pow)
-        ta_p_sq = sbuf([Q, I], F32, "ta_p_sq")
+        ta_p_sq = sbuf([Q, I], F32, "ta_p_sq", "val_pool0")
         sum_ta = sbuf([Q, 1], F32, "sum_ta")
         nc.vector.scalar_tensor_tensor(ta_p_sq[:], ta_bank[:], 1.0, p_sq[:], ALU.mult, ALU.mult, accum_out=sum_ta[:])
         p_unit = sbuf([Q, P, PACK], F32, "p_unit")
@@ -145,29 +147,34 @@ def tile_attend_ttunitweights_kernel(tc, query, keys_words, keys_scales, dquery,
         )
         mean_ta = sbuf([Q, 1], F32, "mean_ta")
         nc.vector.tensor_scalar(mean_ta[:], sum_ta[:], inv_n2[:], inv_n2[:], ALU.mult, ALU.mult)
-        wo = sbuf([Q, I], BF16, "wo", "val_pool1")
+        wo = sbuf([Q, I], BF16, "wo")
         nc.vector.scalar_tensor_tensor(
             wo[:], ta_bank[:], mean_ta[:], p_unit[:].rearrange("q s t -> q (s t)"), ALU.subtract, ALU.mult
         )
-        turned_w = turn(wo, "turned_w", "bank_w")
+        turned_w = turn(wo, "turned_w", "bank_s0")
 
         picked2 = gather_values(2, "p_unit")
         turned2 = turn(picked2, "turned2", "bank_t2")
-        early = sbuf([P, 3, P, 2], F32, "early_grouped", "val_pool2")
-        nc.scalar.copy(early[:, 0, :, :], turned0)
-        nc.scalar.copy(early[:, 1, :, :], turned1)
-        nc.vector.tensor_copy(early[:, 2, :, :], turned_w)
-        early_codes, early_scales = quantize(
-            early[:].rearrange("s n c u -> s (n c u)").bitcast(BF16), 3 * P, "early"
+        codes01, scales01 = quantize(
+            grouped01[:].rearrange("s n c u -> s (n c u)").bitcast(BF16), 2 * P, "v01", "mean_ta"
         )
-        grouped2 = sbuf([P, P, 2], F32, "grouped2")
-        nc.scalar.copy(grouped2[:], turned2)
+
+        picked3 = gather_values(3, "val_pool1")
+        turned3 = turn(picked3, "turned3", "bank_t3")
+
+        grouped_w2 = sbuf([P, 2, P, 2], F32, "grouped_w2", "val_pool3")
+        nc.vector.tensor_copy(grouped_w2[:, 0, :, :], turned_w)
+        nc.scalar.copy(grouped_w2[:, 1, :, :], turned2)
+        codes_w2, scales_w2 = quantize(grouped_w2[:].rearrange("s n c u -> s (n c u)").bitcast(BF16), 2 * P, "w2")
+
+        grouped3 = sbuf([P, P, 2], F32, "grouped3")
+        nc.scalar.copy(grouped3[:], turned3)
 
         def product(bank, codes, scales):
             nc.tensor.matmul_mx(
                 out=bank,
-                lhsT=early_codes[:, 2 * P :].bitcast(FP8X4),
-                lhsT_scale=early_scales[:, 2 * P :],
+                lhsT=codes_w2[:, :P].bitcast(FP8X4),
+                lhsT_scale=scales_w2[:, :P],
                 rhs=codes.bitcast(FP8X4),
                 rhs_scale=scales,
                 start=True,
@@ -175,26 +182,18 @@ def tile_attend_ttunitweights_kernel(tc, query, keys_words, keys_scales, dquery,
             )
 
         bank01 = psum.tile([Q, 2 * P], F32, name="bank01", tag="bank_f")
-        product(bank01[:], early_codes[:, : 2 * P], early_scales[:, : 2 * P])
-
-        picked3 = gather_values(3, "val_pool2")
-        turned3 = turn(picked3, "turned3", "bank_t3")
-        grouped3 = sbuf([P, P, 2], F32, "grouped3")
-        nc.scalar.copy(grouped3[:], turned3)
-
-        codes2, scales2 = quantize(grouped2[:].rearrange("s c u -> s (c u)").bitcast(BF16), P, "v2", "val_pool3")
+        product(bank01[:], codes01[:], scales01[:])
         bank2 = psum.tile([Q, P], F32, name="bank2", tag="bank_s1")
-        product(bank2[:], codes2[:], scales2[:])
-        out01 = sbuf([Q, 2 * P], F32, "out01", "grouped2")
-        nc.vector.tensor_copy(out01[:], bank01[:])
-        nc.sync.dma_start(out[:, : 2 * P], out01[:])
-
+        product(bank2[:], codes_w2[:, P:], scales_w2[:, P:])
         codes3, scales3 = quantize(grouped3[:].rearrange("s c u -> s (c u)").bitcast(BF16), P, "v3")
         bank3 = psum.tile([Q, P], F32, name="bank3")
         product(bank3[:], codes3[:], scales3[:])
+        out01 = sbuf([Q, 2 * P], F32, "out01")
+        nc.scalar.copy(out01[:], bank01[:])
+        nc.sync.dma_start(out[:, : 2 * P], out01[:])
         out2 = sbuf([Q, P], F32, "out2")
         nc.scalar.copy(out2[:], bank2[:])
         nc.sync.dma_start(out[:, 2 * P : 3 * P], out2[:])
         out3 = sbuf([Q, P], F32, "out3")
-        nc.scalar.copy(out3[:], bank3[:])
+        nc.vector.tensor_copy(out3[:], bank3[:])
         nc.sync.dma_start(out[:, 3 * P :], out3[:])

@@ -21,7 +21,7 @@ P = 128
 PACK = 4
 LIST_ROWS = 16
 E_TILES = E // P
-VECTOR_SLOTS = (512, 0, 256, 256)
+VECTOR_SLOTS = (512, 0, 256, 288)
 
 
 def tile_attend_ttunitweights_kernel(tc, query, keys_words, keys_scales, dquery, slot_factor, vals, offs, out):
@@ -52,10 +52,10 @@ def tile_attend_ttunitweights_kernel(tc, query, keys_words, keys_scales, dquery,
         nc.sync.dma_start(key_pool[:].bitcast(I32), keys_words[0].bitcast(I32))
         key_scale_pool = sbuf([P, T], U8, "key_scale_pool")
         nc.vector.memset(key_scale_pool[:].bitcast(I32), 0)
-        for quad in range(4):
+        for r in range(4):
             nc.sync.dma_start(
-                key_scale_pool[32 * quad : 32 * quad + 4, :].bitcast(I32),
-                keys_scales[0, 4 * quad : 4 * quad + 4, :].bitcast(I32),
+                key_scale_pool[r:P:32, :].bitcast(I32),
+                keys_scales[0, r:16:4, :].bitcast(I32),
             )
         q_raw = []
         for n, src in enumerate((query, dquery)):

@@ -21,7 +21,7 @@ P = 128
 PACK = 4
 LIST_ROWS = 16
 E_TILES = E // P
-VECTOR_SLOTS = (512, 0, 256, 288)
+VECTOR_SLOTS = (320, 0, 256, 288)
 
 
 def tile_attend_ttunitweights_kernel(tc, query, keys_words, keys_scales, dquery, slot_factor, vals, offs, out):
@@ -39,11 +39,10 @@ def tile_attend_ttunitweights_kernel(tc, query, keys_words, keys_scales, dquery,
             nc.vector.quantize_mx(out=codes[:].bitcast(FP8X4), scales=scales[:], in_=grouped)
             return codes, scales
 
-        def turn(rows, name, tag):
+        def turn(halves, name, tag):
             bank = psum.tile([P, 2, P], F32, name=name, tag=tag)
-            pairs = rows[:].bitcast(F32)
             for u in range(2):
-                nc.tensor.transpose(bank[:, u, :], pairs[:, u : I // 2 : 2], ident[:])
+                nc.tensor.transpose(bank[:, u, :], halves[u], ident[:])
             return bank[:].rearrange("s u c -> s c u")
 
         offsets = keep.tile([P, I // LIST_ROWS], U16, name="offsets")
@@ -67,8 +66,9 @@ def tile_attend_ttunitweights_kernel(tc, query, keys_words, keys_scales, dquery,
             pool_j = sbuf([P, T], F32, f"val_pool{j}")
             nc.sync.dma_start(pool_j[:], vals[j * P : (j + 1) * P, :])
             val_pool.append(pool_j)
-        factor = sbuf([P, PACK], F32, "factor")
-        nc.gpsimd.dma_start(factor[:], slot_factor[0].rearrange("(s t) -> s t", t=PACK))
+            if j == 0:
+                factor = sbuf([P, PACK], F32, "factor")
+                nc.sync.dma_start(factor[:], slot_factor[0].rearrange("(s t) -> s t", t=PACK))
 
         ident = sbuf([P, P], F32, "ident")
         make_identity(nc, ident[:])
@@ -110,7 +110,8 @@ def tile_attend_ttunitweights_kernel(tc, query, keys_words, keys_scales, dquery,
                 nc.vector.tensor_copy(picked[:, :share], val_pool[j][:].indirect(offsets[:, :cut]))
             if share < I:
                 nc.scalar.activation(picked[:, share:], val_pool[j][:].indirect(offsets[:, cut:]), ACT.Copy)
-            return picked
+            pairs = picked[:].bitcast(F32)
+            return [pairs[:, u : I // 2 : 2] for u in range(2)]
 
         a_m2 = sbuf([Q, I], F32, "a_m2")
         top_m2 = sbuf([Q, 1], F32, "top_m2")
@@ -127,9 +128,9 @@ def tile_attend_ttunitweights_kernel(tc, query, keys_words, keys_scales, dquery,
         turned0 = turn(picked0, "turned0", "bank_s0")
         picked1 = gather_values(1, "a_m2")
         turned1 = turn(picked1, "turned1", "bank_t1")
-        grouped01 = sbuf([P, 2, P, 2], F32, "grouped01", "val_pool1")
-        nc.scalar.copy(grouped01[:, 0, :, :], turned0)
-        nc.scalar.copy(grouped01[:, 1, :, :], turned1)
+        early = sbuf([P, 3, P, 2], F32, "early", "val_pool1")
+        nc.scalar.copy(early[:, 0, :, :], turned0)
+        nc.scalar.copy(early[:, 1, :, :], turned1)
 
         inv_n2 = sbuf([Q, 1], F32, "inv_n2")
         nc.gpsimd.tensor_tensor(inv_n2[:], sum_sq[:], minus_half[:], ALU.pow)
@@ -147,34 +148,28 @@ def tile_attend_ttunitweights_kernel(tc, query, keys_words, keys_scales, dquery,
         )
         mean_ta = sbuf([Q, 1], F32, "mean_ta")
         nc.vector.tensor_scalar(mean_ta[:], sum_ta[:], inv_n2[:], inv_n2[:], ALU.mult, ALU.mult)
-        wo = sbuf([Q, I], BF16, "wo")
-        nc.vector.scalar_tensor_tensor(
-            wo[:], ta_bank[:], mean_ta[:], p_unit[:].rearrange("q s t -> q (s t)"), ALU.subtract, ALU.mult
-        )
-        turned_w = turn(wo, "turned_w", "bank_s0")
+        wo = sbuf([Q, 2, P, 2], BF16, "wo")
+        ta_pairs = ta_bank[:].rearrange("q (s u e) -> q s u e", u=2, e=2)
+        p_pairs = p_unit[:].rearrange("q s (u e) -> q s u e", u=2)
+        for u in range(2):
+            nc.vector.scalar_tensor_tensor(
+                wo[:, u, :, :], ta_pairs[:, :, u, :], mean_ta[:], p_pairs[:, :, u, :], ALU.subtract, ALU.mult
+            )
+        wo_halves = [wo[:, u, :, :].rearrange("q s e -> q (s e)").bitcast(F32) for u in range(2)]
+        turned_w = turn(wo_halves, "turned_w", "bank_s0")
 
         picked2 = gather_values(2, "p_unit")
         turned2 = turn(picked2, "turned2", "bank_t2")
-        codes01, scales01 = quantize(
-            grouped01[:].rearrange("s n c u -> s (n c u)").bitcast(BF16), 2 * P, "v01", "mean_ta"
+        nc.scalar.copy(early[:, 2, :, :], turned_w)
+        early_codes, early_scales = quantize(
+            early[:].rearrange("s n c u -> s (n c u)").bitcast(BF16), 3 * P, "early"
         )
-
-        picked3 = gather_values(3, "val_pool1")
-        turned3 = turn(picked3, "turned3", "bank_t3")
-
-        grouped_w2 = sbuf([P, 2, P, 2], F32, "grouped_w2", "val_pool3")
-        nc.vector.tensor_copy(grouped_w2[:, 0, :, :], turned_w)
-        nc.scalar.copy(grouped_w2[:, 1, :, :], turned2)
-        codes_w2, scales_w2 = quantize(grouped_w2[:].rearrange("s n c u -> s (n c u)").bitcast(BF16), 2 * P, "w2")
-
-        grouped3 = sbuf([P, P, 2], F32, "grouped3")
-        nc.scalar.copy(grouped3[:], turned3)
 
         def product(bank, codes, scales):
             nc.tensor.matmul_mx(
                 out=bank,
-                lhsT=codes_w2[:, :P].bitcast(FP8X4),
-                lhsT_scale=scales_w2[:, :P],
+                lhsT=early_codes[:, 2 * P :].bitcast(FP8X4),
+                lhsT_scale=early_scales[:, 2 * P :],
                 rhs=codes.bitcast(FP8X4),
                 rhs_scale=scales,
                 start=True,
@@ -182,18 +177,29 @@ def tile_attend_ttunitweights_kernel(tc, query, keys_words, keys_scales, dquery,
             )
 
         bank01 = psum.tile([Q, 2 * P], F32, name="bank01", tag="bank_f")
-        product(bank01[:], codes01[:], scales01[:])
-        bank2 = psum.tile([Q, P], F32, name="bank2", tag="bank_s1")
-        product(bank2[:], codes_w2[:, P:], scales_w2[:, P:])
+        product(bank01[:], early_codes[:, : 2 * P], early_scales[:, : 2 * P])
+
+        picked3 = gather_values(3, "val_pool1")
+        turned3 = turn(picked3, "turned3", "bank_t3")
+
+        grouped2 = sbuf([P, P, 2], F32, "grouped2", "val_pool3")
+        nc.scalar.copy(grouped2[:], turned2)
+        codes2, scales2 = quantize(grouped2[:].rearrange("s c u -> s (c u)").bitcast(BF16), P, "v2")
+        out01 = sbuf([Q, 2 * P], F32, "out01", "val_pool3")
+        nc.vector.tensor_copy(out01[:], bank01[:])
+        nc.sync.dma_start(out[:, : 2 * P], out01[:])
+
+        grouped3 = sbuf([P, P, 2], F32, "grouped3")
+        nc.scalar.copy(grouped3[:], turned3)
         codes3, scales3 = quantize(grouped3[:].rearrange("s c u -> s (c u)").bitcast(BF16), P, "v3")
+
+        bank2 = psum.tile([Q, P], F32, name="bank2", tag="bank_s1")
+        product(bank2[:], codes2[:], scales2[:])
         bank3 = psum.tile([Q, P], F32, name="bank3")
         product(bank3[:], codes3[:], scales3[:])
-        out01 = sbuf([Q, 2 * P], F32, "out01")
-        nc.scalar.copy(out01[:], bank01[:])
-        nc.sync.dma_start(out[:, : 2 * P], out01[:])
         out2 = sbuf([Q, P], F32, "out2")
         nc.scalar.copy(out2[:], bank2[:])
         nc.sync.dma_start(out[:, 2 * P : 3 * P], out2[:])
         out3 = sbuf([Q, P], F32, "out3")
-        nc.vector.tensor_copy(out3[:], bank3[:])
-        nc.sync.dma_start(out[:, 3 * P :], out3[:])
+        nc.scalar.copy(out3[:], bank3[:])
+        nc.scalar.dma_start(out[:, 3 * P :], out3[:])

@@ -45,12 +45,13 @@ def tile_attend_ttunitweights_kernel(tc, query, keys_words, keys_scales, dquery,
                 nc.tensor.transpose(bank[:, u, :], halves[u], ident[:])
             return bank[:].rearrange("s u c -> s c u")
 
+        key_scale_pool = sbuf([P, T], U8, "key_scale_pool")
+        nc.vector.memset(key_scale_pool[:, : T // 2].bitcast(I32), 0)
+        nc.gpsimd.memset(key_scale_pool[:, T // 2 :].bitcast(I32), 0)
         offsets = keep.tile([P, I // LIST_ROWS], U16, name="offsets")
         nc.sync.dma_start(offsets[:], offs)
         key_pool = sbuf([P, T], U16, "key_pool")
         nc.sync.dma_start(key_pool[:].bitcast(I32), keys_words[0].bitcast(I32))
-        key_scale_pool = sbuf([P, T], U8, "key_scale_pool")
-        nc.vector.memset(key_scale_pool[:].bitcast(I32), 0)
         for r in range(4):
             nc.sync.dma_start(
                 key_scale_pool[r:P:32, :].bitcast(I32),

from contextlib import ExitStack

import concourse.mybir as mybir
from concourse.masks import make_identity

D, E, T, I, Q = 512, 512, 2048, 512, 128
FLOPS = 2 * Q * I * D * 2 + 2 * Q * I * E

F32 = mybir.dt.float32
BF16 = mybir.dt.bfloat16
I32 = mybir.dt.int32
U32 = mybir.dt.uint32
U16 = mybir.dt.uint16
U8 = mybir.dt.uint8
FP8X4 = mybir.dt.float8_e4m3fn_x4
FP4X4 = mybir.dt.float4_e2m1fn_x4
ALU = mybir.AluOpType
ACT = mybir.ActivationFunctionType

P = 128
PACK = 4
LIST_ROWS = 16
E_TILES = E // P
VECTOR_SLOTS = (320, 0, 256, 288)


def tile_attend_ttunitweights_kernel(tc, query, keys_words, keys_scales, dquery, slot_factor, vals, offs, out):
    nc = tc.nc
    with ExitStack() as ctx:
        keep = ctx.enter_context(tc.tile_pool(name="keep", bufs=1))
        psum = ctx.enter_context(tc.psum_pool(name="psum", bufs=1))

        def sbuf(shape, dtype, name, tag=None):
            return keep.tile(shape, dtype, name=name, tag=tag or name, align_bytes=64)

        def quantize(grouped, columns, name, tag=None):
            codes = sbuf([P, columns], U32, name + "_codes", tag)
            scales = sbuf([P, columns], U8, name + "_scales")
            nc.vector.quantize_mx(out=codes[:].bitcast(FP8X4), scales=scales[:], in_=grouped)
            return codes, scales

        def turn(halves, name, tag):
            bank = psum.tile([P, 2, P], F32, name=name, tag=tag)
            for u in range(2):
                nc.tensor.transpose(bank[:, u, :], halves[u], ident[:])
            return bank[:].rearrange("s u c -> s c u")

        key_scale_pool = sbuf([P, T], U8, "key_scale_pool")
        nc.vector.memset(key_scale_pool[:, : T // 2].bitcast(I32), 0)
        nc.gpsimd.memset(key_scale_pool[:, T // 2 :].bitcast(I32), 0)
        offsets = keep.tile([P, I // LIST_ROWS], U16, name="offsets")
        nc.sync.dma_start(offsets[:], offs)
        key_pool = sbuf([P, T], U16, "key_pool")
        nc.sync.dma_start(key_pool[:].bitcast(I32), keys_words[0].bitcast(I32))
        for r in range(4):
            nc.sync.dma_start(
                key_scale_pool[r:P:32, :].bitcast(I32),
                keys_scales[0, r:16:4, :].bitcast(I32),
            )
        q_raw = []
        for n, src in enumerate((query, dquery)):
            raw = sbuf([P, PACK, Q], F32, f"q_raw{n}")
            nc.sync.dma_start(raw[:], src.rearrange("(p t) q -> p t q", t=PACK))
            q_raw.append(raw)
        val_pool = []
        for j in range(E_TILES):
            pool_j = sbuf([P, T], F32, f"val_pool{j}")
            nc.sync.dma_start(pool_j[:], vals[j * P : (j + 1) * P, :])
            val_pool.append(pool_j)
            if j == 0:
                factor = sbuf([P, PACK], F32, "factor")
                nc.sync.dma_start(factor[:], slot_factor[0].rearrange("(s t) -> s t", t=PACK))

        ident = sbuf([P, P], F32, "ident")
        make_identity(nc, ident[:])
        minus_half = sbuf([P, 1], F32, "minus_half")
        nc.gpsimd.memset(minus_half[:], -0.5)

        factor_bank = psum.tile([Q, PACK, P], F32, name="factor_bank", tag="bank_f")
        for t in range(PACK):
            nc.tensor.transpose(factor_bank[:, t, :], factor[:, t : t + 1].to_broadcast([P, Q]), ident[:])

        key_words = sbuf([P, I], U16, "key_words")
        nc.vector.tensor_copy(key_words[:], key_pool[:].indirect(offsets[:]))
        key_scales = sbuf([P, I], U8, "key_scales")
        nc.vector.tensor_copy(key_scales[:], key_scale_pool[:].indirect(offsets[:]))

        banks = []
        for n in range(2):
            q_grouped = sbuf([P, Q, PACK], BF16, f"q_grouped{n}")
            nc.scalar.copy(q_grouped[:], q_raw[n][:].rearrange("p t q -> p q t"))
            q_codes, q_scales = quantize(q_grouped[:].rearrange("p q t -> p (q t)"), Q, f"q{n}")
            bank = psum.tile([Q, I], F32, name=f"score{n}", tag=f"bank_s{n}")
            nc.tensor.matmul_mx(
                out=bank[:],
                lhsT=q_codes[:].bitcast(FP8X4),
                lhsT_scale=q_scales[:],
                rhs=key_words[:].bitcast(FP4X4),
                rhs_scale=key_scales[:],
                start=True,
                stop=True,
            )
            banks.append(bank)
        a_bank, ta_bank = banks

        def gather_values(j, tag):
            picked = sbuf([P, I], BF16, f"picked{j}", tag)
            share = VECTOR_SLOTS[j]
            cut = share // LIST_ROWS
            if share > 0:
                nc.vector.tensor_copy(picked[:, :share], val_pool[j][:].indirect(offsets[:, :cut]))
            if share < I:
                nc.scalar.activation(picked[:, share:], val_pool[j][:].indirect(offsets[:, cut:]), ACT.Copy)
            pairs = picked[:].bitcast(F32)
            return [pairs[:, u : I // 2 : 2] for u in range(2)]

        a_m2 = sbuf([Q, I], F32, "a_m2")
        top_m2 = sbuf([Q, 1], F32, "top_m2")
        nc.vector.tensor_scalar(a_m2[:], a_bank[:], -2.0, None, ALU.mult, ALU.min, accum_out=top_m2[:])
        p_sq = sbuf([Q, I], F32, "p_sq")
        sum_sq = sbuf([Q, 1], F32, "sum_sq")
        nc.scalar.activation(p_sq[:], a_m2[:], ACT.Exp, bias=top_m2[:], scale=-1.0, accum_out=sum_sq[:])
        top_m1 = sbuf([Q, 1], F32, "top_m1")
        nc.vector.tensor_scalar(top_m1[:], top_m2[:], 0.5, None, ALU.mult)
        p = sbuf([Q, I], F32, "p")
        nc.scalar.activation(p[:], a_m2[:], ACT.Exp, bias=top_m1[:], scale=-0.5)

        picked0 = gather_values(0, "key_words")
        turned0 = turn(picked0, "turned0", "bank_s0")
        picked1 = gather_values(1, "a_m2")
        turned1 = turn(picked1, "turned1", "bank_t1")
        early = sbuf([P, 3, P, 2], F32, "early", "val_pool1")
        nc.scalar.copy(early[:, 0, :, :], turned0)
        nc.scalar.copy(early[:, 1, :, :], turned1)

        inv_n2 = sbuf([Q, 1], F32, "inv_n2")
        nc.gpsimd.tensor_tensor(inv_n2[:], sum_sq[:], minus_half[:], ALU.pow)
        ta_p_sq = sbuf([Q, I], F32, "ta_p_sq", "val_pool0")
        sum_ta = sbuf([Q, 1], F32, "sum_ta")
        nc.vector.scalar_tensor_tensor(ta_p_sq[:], ta_bank[:], 1.0, p_sq[:], ALU.mult, ALU.mult, accum_out=sum_ta[:])
        p_unit = sbuf([Q, P, PACK], F32, "p_unit")
        nc.vector.scalar_tensor_tensor(
            p_unit[:],
            p[:].rearrange("q (s t) -> q s t", t=PACK),
            inv_n2[:],
            factor_bank[:].rearrange("q t s -> q s t"),
            ALU.mult,
            ALU.mult,
        )
        mean_ta = sbuf([Q, 1], F32, "mean_ta")
        nc.vector.tensor_scalar(mean_ta[:], sum_ta[:], inv_n2[:], inv_n2[:], ALU.mult, ALU.mult)
        wo = sbuf([Q, 2, P, 2], BF16, "wo")
        ta_pairs = ta_bank[:].rearrange("q (s u e) -> q s u e", u=2, e=2)
        p_pairs = p_unit[:].rearrange("q s (u e) -> q s u e", u=2)
        for u in range(2):
            nc.vector.scalar_tensor_tensor(
                wo[:, u, :, :], ta_pairs[:, :, u, :], mean_ta[:], p_pairs[:, :, u, :], ALU.subtract, ALU.mult
            )
        wo_halves = [wo[:, u, :, :].rearrange("q s e -> q (s e)").bitcast(F32) for u in range(2)]
        turned_w = turn(wo_halves, "turned_w", "bank_s0")

        picked2 = gather_values(2, "p_unit")
        turned2 = turn(picked2, "turned2", "bank_t2")
        nc.scalar.copy(early[:, 2, :, :], turned_w)
        early_codes, early_scales = quantize(
            early[:].rearrange("s n c u -> s (n c u)").bitcast(BF16), 3 * P, "early"
        )

        def product(bank, codes, scales):
            nc.tensor.matmul_mx(
                out=bank,
                lhsT=early_codes[:, 2 * P :].bitcast(FP8X4),
                lhsT_scale=early_scales[:, 2 * P :],
                rhs=codes.bitcast(FP8X4),
                rhs_scale=scales,
                start=True,
                stop=True,
            )

        bank01 = psum.tile([Q, 2 * P], F32, name="bank01", tag="bank_f")
        product(bank01[:], early_codes[:, : 2 * P], early_scales[:, : 2 * P])

        picked3 = gather_values(3, "val_pool1")
        turned3 = turn(picked3, "turned3", "bank_t3")

        grouped2 = sbuf([P, P, 2], F32, "grouped2", "val_pool3")
        nc.scalar.copy(grouped2[:], turned2)
        codes2, scales2 = quantize(grouped2[:].rearrange("s c u -> s (c u)").bitcast(BF16), P, "v2")
        out01 = sbuf([Q, 2 * P], F32, "out01", "val_pool3")
        nc.vector.tensor_copy(out01[:], bank01[:])
        nc.sync.dma_start(out[:, : 2 * P], out01[:])

        grouped3 = sbuf([P, P, 2], F32, "grouped3")
        nc.scalar.copy(grouped3[:], turned3)
        codes3, scales3 = quantize(grouped3[:].rearrange("s c u -> s (c u)").bitcast(BF16), P, "v3")

        bank2 = psum.tile([Q, P], F32, name="bank2", tag="bank_s1")
        product(bank2[:], codes2[:], scales2[:])
        bank3 = psum.tile([Q, P], F32, name="bank3")
        product(bank3[:], codes3[:], scales3[:])
        out2 = sbuf([Q, P], F32, "out2")
        nc.scalar.copy(out2[:], bank2[:])
        nc.sync.dma_start(out[:, 2 * P : 3 * P], out2[:])
        out3 = sbuf([Q, P], F32, "out3")
        nc.scalar.copy(out3[:], bank3[:])
        nc.scalar.dma_start(out[:, 3 * P :], out3[:])
